import numpy as np
import ml_dtypes


def mxq(x, axis, fmt="e4m3"):
    dtype, down = {"e4m3": (ml_dtypes.float8_e4m3fn, 7), "e5m2": (ml_dtypes.float8_e5m2, 14)}[fmt]
    v = np.moveaxis(np.asarray(x, np.float32).astype(ml_dtypes.bfloat16).astype(np.float64), axis, -1)
    blocks = v.reshape(v.shape[:-1] + (-1, 32))
    amax = np.abs(blocks).max(-1, keepdims=True)
    byte = np.maximum(np.where(amax > 0, np.frexp(amax)[1] - 1 + 127, 0) - down, 1)
    scale = np.exp2(byte - 127.0)
    codes = (blocks / scale).astype(np.float32).astype(dtype).astype(np.float64)
    return np.moveaxis((codes * scale).reshape(v.shape), -1, axis)


WIDE = False


def mx_kscale(k):
    if not WIDE:
        return np.ones(k)
    levels = np.array([10, -10, 5, -5, 0])
    if k % 512:
        return np.exp2(np.random.permutation(np.resize(levels, k // 32))).repeat(32)
    a = np.empty((k // 512, 16))
    for p in range(k // 512):
        a[p, :8] = np.random.permutation(np.resize(levels, 8))
        for g in range(8):
            far = levels[np.abs(levels - a[p, g]) >= 10]
            a[p, g + 8] = far[np.random.randint(len(far))]
    return np.exp2(a.ravel()).repeat(32)


def f64(x):
    return np.asarray(x).astype(np.float64)


def striped(idx):
    return np.tile(idx.reshape(-1, 16).T, (8, 1)).astype(np.uint16)


def unstriped(offs):
    return offs[:16].T.reshape(-1).astype(np.int64)


def striped8(idx):
    return np.concatenate([x.reshape(-1, 16).T for x in idx]).astype(np.uint16)


def runs(offs, k):
    lists = np.stack([offs[16 * r : 16 * r + 16].T.reshape(-1) for r in range(8)]).astype(np.int64)
    return lists[np.arange(k) % 512 // 64]


def pack_weight(w):
    k, n = w.shape
    w = f64(np.asarray(w, np.float32).astype(ml_dtypes.bfloat16)).reshape(k // 32, 32, n)
    amax = np.abs(w).max(1)
    byte = np.clip(np.where(amax > 0, np.frexp(amax)[1] - 1 + 127 - 7, 1), 1, 254)
    scaled = (w * np.exp2(127.0 - byte)[:, None, :]).reshape(k, n).astype(np.float32)
    words = np.ascontiguousarray(scaled.reshape(k // 512, 128, 4, n).transpose(0, 1, 3, 2)).astype(ml_dtypes.float8_e4m3fn).view(np.uint8)
    return words, np.ascontiguousarray(byte.astype(np.uint8).reshape(k // 512, 16, n))


def unpack_weight(words, scales):
    g, p, n, _ = words.shape
    vals = np.ascontiguousarray(words).view(ml_dtypes.float8_e4m3fn).astype(np.float64) * np.repeat(np.exp2(scales.astype(np.float64) - 127.0), 8, axis=1)[..., None]
    return vals.transpose(0, 1, 3, 2).reshape(g * 512, n)


def silu(v):
    return v / (1.0 + np.exp(-np.maximum(v, -700.0)))


K, T, S, V, N, H = 512, 2048, 512, 256, 512, 512


def setup_inputs():
    n = np.random.standard_normal
    s = mx_kscale(K)[:, None]
    u = mx_kscale(H)
    packed_xT = pack_weight(n((K, T)) * s)
    return {
        "x_words": packed_xT[0],
        "x_scales": packed_xT[1],
        "w1": (n((K, H)) / np.sqrt(K) / s * u).astype(np.float32),
        "wt": np.repeat(np.random.uniform(0.3, 1.2, (8, V)), 64, axis=0).astype(np.float32),
        "w2": (n((H, N)) / np.sqrt(H) / u[:, None]).astype(np.float32),
        "offs": striped(np.random.permutation(T)[:S]),
        "take": striped8(np.stack([np.random.permutation(S)[:V] for _ in range(8)])),
    }


def reference(x_words, x_scales, w1, wt, w2, offs, take):
    xq = unpack_weight(x_words, x_scales)[:, unstriped(offs)]
    y = mxq(f64(w1), 0, "e4m3").T @ xq
    e = (silu(y[np.arange(H)[:, None], runs(take, H)])) * f64(wt)
    z = np.zeros((H, S))
    z[np.arange(H)[:, None], runs(take, H)] = e
    return mxq(f64(w2), 0, "e4m3").T @ mxq(z, 0, "e4m3")

@@ -1,0 +1,147 @@
+from contextlib import ExitStack
+
+import concourse.mybir as mybir
+
+K, T, S, V, N, H = 512, 2048, 512, 256, 512, 512
+FLOPS = 2 * K * H * S + 2 * H * N * S
+BYTES = K * T + (K // 32) * T + 4 * K * H + 4 * 8 * V + 4 * H * N + 2 * 128 * (S + V) // 16 + 4 * N * S
+
+F32 = mybir.dt.float32
+BF16 = mybir.dt.bfloat16
+I32 = mybir.dt.int32
+U32 = mybir.dt.uint32
+U16 = mybir.dt.uint16
+U8 = mybir.dt.uint8
+FP8X4 = mybir.dt.float8_e4m3fn_x4
+SILU = mybir.ActivationFunctionType.Silu
+MULT = mybir.AluOpType.mult
+
+P = 128
+PACK = 4
+HALF = S // 2
+W1_VECTOR_M = 80
+CHUNKS = ((0, 128), (128, 256), (384, 128))
+
+
+def tile_picked_echoice_silu_p_kernel(tc, x_words, x_scales, w1, wt, w2, offs, take, out):
+    nc = tc.nc
+    with ExitStack() as ctx:
+        lists = ctx.enter_context(tc.tile_pool(name="lists", bufs=1))
+        sb = ctx.enter_context(tc.tile_pool(name="sb", bufs=1))
+        psum = ctx.enter_context(tc.psum_pool(name="psum", bufs=1))
+
+        def mx(acc, lhs_codes, lhs_scales, rhs_codes, rhs_scales):
+            nc.tensor.matmul_mx(out=acc, lhsT=lhs_codes.bitcast(FP8X4), lhsT_scale=lhs_scales,
+                                rhs=rhs_codes.bitcast(FP8X4), rhs_scale=rhs_scales, start=True, stop=True)
+
+        def quantize(codes, scales, grouped):
+            nc.vector.quantize_mx(out=codes.bitcast(FP8X4), scales=scales, in_=grouped)
+
+        def interleave(engine_copy, grouped, planes):
+            engine_copy(out=grouped.rearrange("p (c i t) -> p c t i", i=4, t=PACK),
+                        in_=planes.rearrange("p t (c i) -> p c t i", i=4))
+
+        offs_sb = lists.tile([P, S // 16], U16, name="offs_sb")
+        take_sb = lists.tile([P, V // 16], U16, name="take_sb")
+        scale_table = sb.tile([P, T], U8, name="scale_table", align_bytes=64)
+        w1_raw = sb.tile([P, PACK, H], F32, name="w1_raw", tag="w_raw", align_bytes=64)
+
+        nc.vector.memset(scale_table[:].bitcast(I32), 0)
+        nc.scalar.dma_start(w1_raw[:], w1.rearrange("(p j) c -> p j c", j=PACK))
+        nc.sync.dma_start(offs_sb[:], offs)
+        nc.sync.dma_start(take_sb[:], take)
+        for q in range(4):
+            nc.sync.dma_start(scale_table[32 * q : 32 * q + 4, :].bitcast(I32), x_scales[0, 4 * q : 4 * q + 4, :].bitcast(I32))
+
+        warm_in = sb.tile([P, 8], F32, name="warm_in", tag="words_then_wt", align_bytes=64)
+        warm_out = sb.tile([P, 8], F32, name="warm_out")
+        nc.gpsimd.memset(warm_in[:], 0.0)
+        nc.scalar.activation(warm_out[:], warm_in[:], SILU)
+        word_table = sb.tile([P, T], U32, name="word_table", tag="words_then_wt", align_bytes=64)
+        nc.sync.dma_start(word_table[:].bitcast(I32), x_words[0].rearrange("p n t -> p (n t)").bitcast(I32))
+
+        z = [sb.tile([P, S], F32, name=f"z{t}", align_bytes=64) for t in range(PACK)]
+        for t in range(PACK):
+            nc.vector.memset(z[t][:], 0.0)
+
+        x_scale = sb.tile([P, S], U8, name="x_scale", align_bytes=64)
+        nc.vector.tensor_copy(x_scale[:], scale_table[:].indirect(offs_sb[:]))
+
+        w1_grouped = sb.tile([P, PACK, P, PACK], BF16, name="w1_grouped", align_bytes=64)
+        w1_dst = w1_grouped[:].rearrange("p t m j -> p m j t")
+        w1_src = w1_raw[:].rearrange("p j (m t) -> p m j t", t=PACK)
+        nc.vector.tensor_copy(out=w1_dst[:, :W1_VECTOR_M], in_=w1_src[:, :W1_VECTOR_M])
+        nc.scalar.copy(out=w1_dst[:, W1_VECTOR_M:], in_=w1_src[:, W1_VECTOR_M:])
+        w1_codes = [sb.tile([P, P], U32, name=f"w1_codes{t}", align_bytes=64) for t in range(PACK)]
+        w1_scales = [sb.tile([P, P], U8, name=f"w1_scales{t}", align_bytes=64) for t in range(PACK)]
+
+        def quantize_w1(t):
+            quantize(w1_codes[t][:], w1_scales[t][:], w1_grouped[:, t].rearrange("p m j -> p (m j)"))
+
+        w2_raw = sb.tile([P, PACK, N], F32, name="w2_raw", tag="w_raw", align_bytes=64)
+        nc.sync.dma_start(w2_raw[:], w2.rearrange("(p j) c -> p j c", j=PACK))
+
+        quantize_w1(0)
+        x_codes = [sb.tile([P, HALF], U32, name=f"x_codes{h}", align_bytes=64) for h in range(2)]
+        for h in range(2):
+            nc.vector.tensor_copy(x_codes[h][:], word_table[:].indirect(offs_sb[:, h * HALF // 16 : (h + 1) * HALF // 16]))
+        for t in range(1, PACK):
+            quantize_w1(t)
+
+        wt_sb = sb.tile([P, V], F32, name="wt_sb", tag="words_then_wt", align_bytes=64)
+        nc.sync.dma_start(wt_sb[:], wt.rearrange("(p j) v -> p j v", j=PACK)[:, 0, :])
+
+        act = [sb.tile([P, S], F32, name=f"act{t}", align_bytes=64) for t in range(PACK)]
+        for t in range(PACK):
+            for h in range(2):
+                cols = slice(h * HALF, (h + 1) * HALF)
+                y = psum.tile([P, HALF], F32, name=f"y{t}{h}", tag=f"bank{2 * t + h}")
+                mx(y[:], w1_codes[t][:], w1_scales[t][:], x_codes[h][:], x_scale[:, cols])
+                nc.scalar.activation(act[t][:, cols], y[:], SILU)
+
+        taken = [sb.tile([P, V], F32, name=f"taken{t}", align_bytes=64) for t in range(PACK)]
+        for t in range(PACK):
+            nc.vector.tensor_copy(taken[t][:], act[t][:].indirect(take_sb[:]))
+
+        w2_grouped = [sb.tile([P, PACK * N // 2], BF16, name=f"w2_grouped{h}", align_bytes=64) for h in range(2)]
+        for h in range(2):
+            interleave(nc.scalar.copy, w2_grouped[h][:], w2_raw[:, :, h * N // 2 : (h + 1) * N // 2])
+
+        planes = [sb.tile([P, PACK, width], BF16, name=f"planes{c}", align_bytes=64) for c, (c0, width) in enumerate(CHUNKS)]
+        for t in range(PACK):
+            nc.vector.tensor_tensor(z[t][:].indirect(take_sb[:]), taken[t][:], wt_sb[:], MULT)
+            for c, (c0, width) in enumerate(CHUNKS):
+                nc.scalar.copy(out=planes[c][:, t, :], in_=z[t][:, c0 : c0 + width])
+
+        w2_codes = [sb.tile([P, N // 2], U32, name=f"w2_codes{h}", align_bytes=64) for h in range(2)]
+        w2_scales = [sb.tile([P, N // 2], U8, name=f"w2_scales{h}", align_bytes=64) for h in range(2)]
+        for h in range(2):
+            quantize(w2_codes[h][:], w2_scales[h][:], w2_grouped[h][:])
+
+        z_grouped = [sb.tile([P, PACK * width], BF16, name=f"z_grouped{c}", align_bytes=64) for c, (c0, width) in enumerate(CHUNKS)]
+        z_codes = [sb.tile([P, width], U32, name=f"z_codes{c}", align_bytes=64) for c, (c0, width) in enumerate(CHUNKS)]
+        z_scales = [sb.tile([P, width], U8, name=f"z_scales{c}", align_bytes=64) for c, (c0, width) in enumerate(CHUNKS)]
+        interleave(nc.vector.tensor_copy, z_grouped[0][:], planes[0][:])
+        interleave(nc.scalar.copy, z_grouped[1][:, PACK * P :], planes[1][:, :, P:])
+        interleave(nc.vector.tensor_copy, z_grouped[1][:, : PACK * P], planes[1][:, :, :P])
+        quantize(z_codes[0][:], z_scales[0][:], z_grouped[0][:])
+        interleave(nc.vector.tensor_copy, z_grouped[2][:], planes[2][:])
+        quantize(z_codes[1][:], z_scales[1][:], z_grouped[1][:])
+        quantize(z_codes[2][:], z_scales[2][:], z_grouped[2][:])
+
+        out_rows = out.rearrange("(u p) s -> p u s", p=P)
+        bank = 0
+        for c, (c0, width) in enumerate(CHUNKS):
+            per_bank = HALF // width
+            for u0 in range(0, N // P, per_bank):
+                acc = psum.tile([P, per_bank, width], F32, name=f"acc{bank}", tag=f"bank{bank}")
+                for i in range(per_bank):
+                    h, m0 = divmod((u0 + i) * P, N // 2)
+                    mx(acc[:, i, :], w2_codes[h][:, m0 : m0 + P], w2_scales[h][:, m0 : m0 + P], z_codes[c][:], z_scales[c][:])
+                staged = sb.tile([P, per_bank, width], F32, name=f"staged{bank}")
+                if bank < 2 or bank % 2 == 0:
+                    nc.scalar.copy(out=staged[:], in_=acc[:])
+                else:
+                    nc.vector.tensor_copy(out=staged[:], in_=acc[:])
+                nc.sync.dma_start(out_rows[:, u0 : u0 + per_bank, c0 : c0 + width], staged[:])
+                bank = bank + 1

@@ -19,8 +19,10 @@ MULT = mybir.AluOpType.mult
 P = 128
 PACK = 4
 HALF = S // 2
-W1_VECTOR_M = 80
-CHUNKS = ((0, 128), (128, 256), (384, 128))
+W1_VECTOR_M = 48
+LAST_VECTOR_COLS = 192
+CHUNKS = ((0, 128), (128, 128), (256, 256))
+Y_PIECES = ((0, 0, 256), (1, 0, 256), (0, 256, 128), (0, 384, 128), (1, 256, 256), (2, 0, 512), (3, 0, 256), (3, 256, 256))
 
 
 def tile_picked_echoice_silu_p_kernel(tc, x_words, x_scales, w1, wt, w2, offs, take, out):
@@ -43,8 +45,8 @@ def tile_picked_echoice_silu_p_kernel(tc, x_words, x_scales, w1, wt, w2, offs, t
 
         offs_sb = lists.tile([P, S // 16], U16, name="offs_sb")
         take_sb = lists.tile([P, V // 16], U16, name="take_sb")
-        scale_table = sb.tile([P, T], U8, name="scale_table", align_bytes=64)
-        w1_raw = sb.tile([P, PACK, H], F32, name="w1_raw", tag="w_raw", align_bytes=64)
+        scale_table = sb.tile([P, T], U8, name="scale_table", tag="scales_then_wt", align_bytes=64)
+        w1_raw = sb.tile([P, PACK, H], F32, name="w1_raw", align_bytes=64)
 
         nc.vector.memset(scale_table[:].bitcast(I32), 0)
         nc.scalar.dma_start(w1_raw[:], w1.rearrange("(p j) c -> p j c", j=PACK))
@@ -53,16 +55,19 @@ def tile_picked_echoice_silu_p_kernel(tc, x_words, x_scales, w1, wt, w2, offs, t
         for q in range(4):
             nc.sync.dma_start(scale_table[32 * q : 32 * q + 4, :].bitcast(I32), x_scales[0, 4 * q : 4 * q + 4, :].bitcast(I32))
 
-        warm_in = sb.tile([P, 8], F32, name="warm_in", tag="words_then_wt", align_bytes=64)
+        warm_in = sb.tile([P, 8], F32, name="warm_in", tag="warm_then_w2", align_bytes=64)
         warm_out = sb.tile([P, 8], F32, name="warm_out")
         nc.gpsimd.memset(warm_in[:], 0.0)
         nc.scalar.activation(warm_out[:], warm_in[:], SILU)
-        word_table = sb.tile([P, T], U32, name="word_table", tag="words_then_wt", align_bytes=64)
-        nc.sync.dma_start(word_table[:].bitcast(I32), x_words[0].rearrange("p n t -> p (n t)").bitcast(I32))
 
-        z = [sb.tile([P, S], F32, name=f"z{t}", align_bytes=64) for t in range(PACK)]
-        for t in range(PACK):
+        z = [sb.tile([P, S], F32, name=f"z{t}", tag=f"z{t}", align_bytes=64) for t in range(PACK)]
+        zeros = sb.tile([P, S], F32, name="zeros", tag="zeros_then_words", align_bytes=64)
+        nc.vector.memset(zeros[:], 0.0)
+        nc.vector.tensor_copy(out=z[0][:], in_=zeros[:])
+        for t in range(1, PACK):
             nc.vector.memset(z[t][:], 0.0)
+        word_table = sb.tile([P, T], U32, name="word_table", tag="zeros_then_words", align_bytes=64)
+        nc.sync.dma_start(word_table[:].bitcast(I32), x_words[0].rearrange("p n t -> p (n t)").bitcast(I32))
 
         x_scale = sb.tile([P, S], U8, name="x_scale", align_bytes=64)
         nc.vector.tensor_copy(x_scale[:], scale_table[:].indirect(offs_sb[:]))
@@ -72,76 +77,91 @@ def tile_picked_echoice_silu_p_kernel(tc, x_words, x_scales, w1, wt, w2, offs, t
         w1_src = w1_raw[:].rearrange("p j (m t) -> p m j t", t=PACK)
         nc.vector.tensor_copy(out=w1_dst[:, :W1_VECTOR_M], in_=w1_src[:, :W1_VECTOR_M])
         nc.scalar.copy(out=w1_dst[:, W1_VECTOR_M:], in_=w1_src[:, W1_VECTOR_M:])
-        w1_codes = [sb.tile([P, P], U32, name=f"w1_codes{t}", align_bytes=64) for t in range(PACK)]
-        w1_scales = [sb.tile([P, P], U8, name=f"w1_scales{t}", align_bytes=64) for t in range(PACK)]
+        w1_codes = sb.tile([P, PACK, P], U32, name="w1_codes", align_bytes=64)
+        w1_scales = sb.tile([P, PACK, P], U8, name="w1_scales", align_bytes=64)
 
-        def quantize_w1(t):
-            quantize(w1_codes[t][:], w1_scales[t][:], w1_grouped[:, t].rearrange("p m j -> p (m j)"))
+        def quantize_w1(h):
+            pair = slice(2 * h, 2 * h + 2)
+            quantize(w1_codes[:, pair, :].rearrange("p t m -> p (t m)"), w1_scales[:, pair, :].rearrange("p t m -> p (t m)"),
+                     w1_grouped[:, pair].rearrange("p t m j -> p (t m j)"))
 
-        w2_raw = sb.tile([P, PACK, N], F32, name="w2_raw", tag="w_raw", align_bytes=64)
+        w2_raw = sb.tile([P, PACK, N], F32, name="w2_raw", tag="warm_then_w2", align_bytes=64)
         nc.sync.dma_start(w2_raw[:], w2.rearrange("(p j) c -> p j c", j=PACK))
 
         quantize_w1(0)
-        x_codes = [sb.tile([P, HALF], U32, name=f"x_codes{h}", align_bytes=64) for h in range(2)]
+        x_codes = sb.tile([P, S], U32, name="x_codes", tag="x_codes_then_w2", align_bytes=64)
         for h in range(2):
-            nc.vector.tensor_copy(x_codes[h][:], word_table[:].indirect(offs_sb[:, h * HALF // 16 : (h + 1) * HALF // 16]))
-        for t in range(1, PACK):
-            quantize_w1(t)
+            nc.vector.tensor_copy(x_codes[:, h * HALF : (h + 1) * HALF], word_table[:].indirect(offs_sb[:, h * HALF // 16 : (h + 1) * HALF // 16]))
+        quantize_w1(1)
 
-        wt_sb = sb.tile([P, V], F32, name="wt_sb", tag="words_then_wt", align_bytes=64)
+        wt_sb = sb.tile([P, V], F32, name="wt_sb", tag="scales_then_wt", align_bytes=64)
         nc.sync.dma_start(wt_sb[:], wt.rearrange("(p j) v -> p j v", j=PACK)[:, 0, :])
 
         act = [sb.tile([P, S], F32, name=f"act{t}", align_bytes=64) for t in range(PACK)]
-        for t in range(PACK):
-            for h in range(2):
-                cols = slice(h * HALF, (h + 1) * HALF)
-                y = psum.tile([P, HALF], F32, name=f"y{t}{h}", tag=f"bank{2 * t + h}")
-                mx(y[:], w1_codes[t][:], w1_scales[t][:], x_codes[h][:], x_scale[:, cols])
-                nc.scalar.activation(act[t][:, cols], y[:], SILU)
+        for bank, (t, c0, width) in enumerate(Y_PIECES):
+            cols = slice(c0, c0 + width)
+            y = psum.tile([P, width], F32, name=f"y{bank}", tag=f"bank{bank}")
+            mx(y[:], w1_codes[:, t, :], w1_scales[:, t, :], x_codes[:, cols], x_scale[:, cols])
+            nc.scalar.activation(act[t][:, cols], y[:], SILU)
 
         taken = [sb.tile([P, V], F32, name=f"taken{t}", align_bytes=64) for t in range(PACK)]
         for t in range(PACK):
             nc.vector.tensor_copy(taken[t][:], act[t][:].indirect(take_sb[:]))
 
-        w2_grouped = [sb.tile([P, PACK * N // 2], BF16, name=f"w2_grouped{h}", align_bytes=64) for h in range(2)]
-        for h in range(2):
-            interleave(nc.scalar.copy, w2_grouped[h][:], w2_raw[:, :, h * N // 2 : (h + 1) * N // 2])
-
-        planes = [sb.tile([P, PACK, width], BF16, name=f"planes{c}", align_bytes=64) for c, (c0, width) in enumerate(CHUNKS)]
-        for t in range(PACK):
-            nc.vector.tensor_tensor(z[t][:].indirect(take_sb[:]), taken[t][:], wt_sb[:], MULT)
-            for c, (c0, width) in enumerate(CHUNKS):
-                nc.scalar.copy(out=planes[c][:, t, :], in_=z[t][:, c0 : c0 + width])
-
+        w2_grouped = [sb.tile([P, PACK * N // 2], BF16, name="w2_grouped0", tag="x_codes_then_w2", align_bytes=64),
+                      sb.tile([P, PACK * N // 2], BF16, name="w2_grouped1", tag="z1", align_bytes=64)]
         w2_codes = [sb.tile([P, N // 2], U32, name=f"w2_codes{h}", align_bytes=64) for h in range(2)]
         w2_scales = [sb.tile([P, N // 2], U8, name=f"w2_scales{h}", align_bytes=64) for h in range(2)]
-        for h in range(2):
-            quantize(w2_codes[h][:], w2_scales[h][:], w2_grouped[h][:])
-
         z_grouped = [sb.tile([P, PACK * width], BF16, name=f"z_grouped{c}", align_bytes=64) for c, (c0, width) in enumerate(CHUNKS)]
         z_codes = [sb.tile([P, width], U32, name=f"z_codes{c}", align_bytes=64) for c, (c0, width) in enumerate(CHUNKS)]
         z_scales = [sb.tile([P, width], U8, name=f"z_scales{c}", align_bytes=64) for c, (c0, width) in enumerate(CHUNKS)]
-        interleave(nc.vector.tensor_copy, z_grouped[0][:], planes[0][:])
-        interleave(nc.scalar.copy, z_grouped[1][:, PACK * P :], planes[1][:, :, P:])
-        interleave(nc.vector.tensor_copy, z_grouped[1][:, : PACK * P], planes[1][:, :, :P])
+        planes = [sb.tile([P, PACK, width], BF16, name=f"planes{c}", align_bytes=64) for c, (c0, width) in enumerate(CHUNKS) if c > 0]
+        first_slots = z_grouped[0][:].rearrange("p (c t) -> p c t", t=PACK)
+
+        def interleave_w2(h):
+            interleave(nc.scalar.copy, w2_grouped[h][:], w2_raw[:, :, h * N // 2 : (h + 1) * N // 2])
+
+        def round_plane(t, c):
+            c0, width = CHUNKS[c]
+            nc.scalar.copy(out=planes[c - 1][:, t, :], in_=z[t][:, c0 : c0 + width])
+
+        for t in range(PACK):
+            nc.vector.tensor_tensor(z[t][:].indirect(take_sb[:]), taken[t][:], wt_sb[:], MULT)
+        interleave_w2(0)
+        for t in (0, 1):
+            nc.scalar.copy(out=first_slots[:, :, t], in_=z[t][:, :P])
+            round_plane(t, 1)
+            round_plane(t, 2)
+        interleave_w2(1)
+        for t in (2, 3):
+            nc.vector.tensor_copy(out=first_slots[:, :, t], in_=z[t][:, :P])
+        round_plane(2, 1)
+        round_plane(2, 2)
+        round_plane(3, 1)
+        interleave(nc.scalar.copy, z_grouped[1][:], planes[0][:])
+        round_plane(3, 2)
+
+        quantize(w2_codes[0][:], w2_scales[0][:], w2_grouped[0][:])
         quantize(z_codes[0][:], z_scales[0][:], z_grouped[0][:])
-        interleave(nc.vector.tensor_copy, z_grouped[2][:], planes[2][:])
+        quantize(w2_codes[1][:], w2_scales[1][:], w2_grouped[1][:])
         quantize(z_codes[1][:], z_scales[1][:], z_grouped[1][:])
+        interleave(nc.scalar.copy, z_grouped[2][:, PACK * LAST_VECTOR_COLS :], planes[1][:, :, LAST_VECTOR_COLS:])
+        interleave(nc.vector.tensor_copy, z_grouped[2][:, : PACK * LAST_VECTOR_COLS], planes[1][:, :, :LAST_VECTOR_COLS])
         quantize(z_codes[2][:], z_scales[2][:], z_grouped[2][:])
 
         out_rows = out.rearrange("(u p) s -> p u s", p=P)
-        bank = 0
-        for c, (c0, width) in enumerate(CHUNKS):
-            per_bank = HALF // width
-            for u0 in range(0, N // P, per_bank):
-                acc = psum.tile([P, per_bank, width], F32, name=f"acc{bank}", tag=f"bank{bank}")
-                for i in range(per_bank):
-                    h, m0 = divmod((u0 + i) * P, N // 2)
-                    mx(acc[:, i, :], w2_codes[h][:, m0 : m0 + P], w2_scales[h][:, m0 : m0 + P], z_codes[c][:], z_scales[c][:])
-                staged = sb.tile([P, per_bank, width], F32, name=f"staged{bank}")
-                if bank < 2 or bank % 2 == 0:
-                    nc.scalar.copy(out=staged[:], in_=acc[:])
-                else:
-                    nc.vector.tensor_copy(out=staged[:], in_=acc[:])
-                nc.sync.dma_start(out_rows[:, u0 : u0 + per_bank, c0 : c0 + width], staged[:])
-                bank = bank + 1
+        pieces = [(0, 0, 2, 0, P), (0, 2, 2, 0, P), (1, 0, 2, 0, P), (1, 2, 2, 0, P),
+                  (2, 0, 1, 0, HALF), (2, 1, 1, 0, HALF), (2, 2, 1, 0, HALF), (2, 3, 1, 0, P), (2, 3, 1, P, P)]
+        for n, (c, u0, tiles, lo, width) in enumerate(pieces):
+            acc = psum.tile([P, tiles, width], F32, name=f"acc{n}", tag=f"bank{n % 8}")
+            for i in range(tiles):
+                h, m0 = divmod((u0 + i) * P, N // 2)
+                mx(acc[:, i, :], w2_codes[h][:, m0 : m0 + P], w2_scales[h][:, m0 : m0 + P],
+                   z_codes[c][:, lo : lo + width], z_scales[c][:, lo : lo + width])
+            staged = sb.tile([P, tiles, width], F32, name=f"staged{n}")
+            if n < 3 or n % 2 == 0:
+                nc.scalar.copy(out=staged[:], in_=acc[:])
+            else:
+                nc.vector.tensor_copy(out=staged[:], in_=acc[:])
+            c0 = CHUNKS[c][0] + lo
+            nc.sync.dma_start(out_rows[:, u0 : u0 + tiles, c0 : c0 + width], staged[:])

@@ -19,7 +19,7 @@ MULT = mybir.AluOpType.mult
 P = 128
 PACK = 4
 HALF = S // 2
-W1_VECTOR_M = 48
+W1_VECTOR_M = 64
 LAST_VECTOR_COLS = 192
 CHUNKS = ((0, 128), (128, 128), (256, 256))
 Y_PIECES = ((0, 0, 256), (1, 0, 256), (0, 256, 128), (0, 384, 128), (1, 256, 256), (2, 0, 512), (3, 0, 256), (3, 256, 256))
@@ -75,14 +75,16 @@ def tile_picked_echoice_silu_p_kernel(tc, x_words, x_scales, w1, wt, w2, offs, t
         w1_grouped = sb.tile([P, PACK, P, PACK], BF16, name="w1_grouped", align_bytes=64)
         w1_dst = w1_grouped[:].rearrange("p t m j -> p m j t")
         w1_src = w1_raw[:].rearrange("p j (m t) -> p m j t", t=PACK)
-        nc.vector.tensor_copy(out=w1_dst[:, :W1_VECTOR_M], in_=w1_src[:, :W1_VECTOR_M])
-        nc.scalar.copy(out=w1_dst[:, W1_VECTOR_M:], in_=w1_src[:, W1_VECTOR_M:])
-        w1_codes = sb.tile([P, PACK, P], U32, name="w1_codes", align_bytes=64)
+        nc.vector.tensor_copy(out=w1_dst[:, :W1_VECTOR_M, :, :2], in_=w1_src[:, :W1_VECTOR_M, :, :2])
+        nc.scalar.copy(out=w1_dst[:, W1_VECTOR_M:, :, :2], in_=w1_src[:, W1_VECTOR_M:, :, :2])
+        nc.scalar.copy(out=w1_dst[:, :, :, 2:], in_=w1_src[:, :, :, 2:])
+        w1_codes = [sb.tile([P, 2, P], U32, name="w1_codes0", align_bytes=64),
+                    sb.tile([P, 2, P], U32, name="w1_codes1", tag="zeros_then_words", align_bytes=64)]
         w1_scales = sb.tile([P, PACK, P], U8, name="w1_scales", align_bytes=64)
 
         def quantize_w1(h):
             pair = slice(2 * h, 2 * h + 2)
-            quantize(w1_codes[:, pair, :].rearrange("p t m -> p (t m)"), w1_scales[:, pair, :].rearrange("p t m -> p (t m)"),
+            quantize(w1_codes[h][:].rearrange("p t m -> p (t m)"), w1_scales[:, pair, :].rearrange("p t m -> p (t m)"),
                      w1_grouped[:, pair].rearrange("p t m j -> p (t m j)"))
 
         w2_raw = sb.tile([P, PACK, N], F32, name="w2_raw", tag="warm_then_w2", align_bytes=64)
@@ -101,7 +103,7 @@ def tile_picked_echoice_silu_p_kernel(tc, x_words, x_scales, w1, wt, w2, offs, t
         for bank, (t, c0, width) in enumerate(Y_PIECES):
             cols = slice(c0, c0 + width)
             y = psum.tile([P, width], F32, name=f"y{bank}", tag=f"bank{bank}")
-            mx(y[:], w1_codes[:, t, :], w1_scales[:, t, :], x_codes[:, cols], x_scale[:, cols])
+            mx(y[:], w1_codes[t // 2][:, t % 2, :], w1_scales[:, t, :], x_codes[:, cols], x_scale[:, cols])
             nc.scalar.activation(act[t][:, cols], y[:], SILU)
 
         taken = [sb.tile([P, V], F32, name=f"taken{t}", align_bytes=64) for t in range(PACK)]
@@ -150,7 +152,7 @@ def tile_picked_echoice_silu_p_kernel(tc, x_words, x_scales, w1, wt, w2, offs, t
         quantize(z_codes[2][:], z_scales[2][:], z_grouped[2][:])
 
         out_rows = out.rearrange("(u p) s -> p u s", p=P)
-        pieces = [(0, 0, 2, 0, P), (0, 2, 2, 0, P), (1, 0, 2, 0, P), (1, 2, 2, 0, P),
+        pieces = [(0, 0, 1, 0, P), (0, 1, 1, 0, P), (0, 2, 2, 0, P), (1, 0, 2, 0, P), (1, 2, 2, 0, P),
                   (2, 0, 1, 0, HALF), (2, 1, 1, 0, HALF), (2, 2, 1, 0, HALF), (2, 3, 1, 0, P), (2, 3, 1, P, P)]
         for n, (c, u0, tiles, lo, width) in enumerate(pieces):
             acc = psum.tile([P, tiles, width], F32, name=f"acc{n}", tag=f"bank{n % 8}")
@@ -159,7 +161,7 @@ def tile_picked_echoice_silu_p_kernel(tc, x_words, x_scales, w1, wt, w2, offs, t
                 mx(acc[:, i, :], w2_codes[h][:, m0 : m0 + P], w2_scales[h][:, m0 : m0 + P],
                    z_codes[c][:, lo : lo + width], z_scales[c][:, lo : lo + width])
             staged = sb.tile([P, tiles, width], F32, name=f"staged{n}")
-            if n < 3 or n % 2 == 0:
+            if n < 4 or n % 2 == 1:
                 nc.scalar.copy(out=staged[:], in_=acc[:])
             else:
                 nc.vector.tensor_copy(out=staged[:], in_=acc[:])

from contextlib import ExitStack

import concourse.mybir as mybir

K, T, S, V, N, H = 512, 2048, 512, 256, 512, 512
FLOPS = 2 * K * H * S + 2 * H * N * S
BYTES = K * T + (K // 32) * T + 4 * K * H + 4 * 8 * V + 4 * H * N + 2 * 128 * (S + V) // 16 + 4 * N * S

F32 = mybir.dt.float32
BF16 = mybir.dt.bfloat16
I32 = mybir.dt.int32
U32 = mybir.dt.uint32
U16 = mybir.dt.uint16
U8 = mybir.dt.uint8
FP8X4 = mybir.dt.float8_e4m3fn_x4
SILU = mybir.ActivationFunctionType.Silu
MULT = mybir.AluOpType.mult

P = 128
PACK = 4
HALF = S // 2
W1_VECTOR_M = 64
LAST_VECTOR_COLS = 192
CHUNKS = ((0, 128), (128, 128), (256, 256))
Y_PIECES = ((0, 0, 256), (1, 0, 256), (0, 256, 128), (0, 384, 128), (1, 256, 256), (2, 0, 512), (3, 0, 256), (3, 256, 256))


def tile_picked_echoice_silu_p_kernel(tc, x_words, x_scales, w1, wt, w2, offs, take, out):
    nc = tc.nc
    with ExitStack() as ctx:
        lists = ctx.enter_context(tc.tile_pool(name="lists", bufs=1))
        sb = ctx.enter_context(tc.tile_pool(name="sb", bufs=1))
        psum = ctx.enter_context(tc.psum_pool(name="psum", bufs=1))

        def mx(acc, lhs_codes, lhs_scales, rhs_codes, rhs_scales):
            nc.tensor.matmul_mx(out=acc, lhsT=lhs_codes.bitcast(FP8X4), lhsT_scale=lhs_scales,
                                rhs=rhs_codes.bitcast(FP8X4), rhs_scale=rhs_scales, start=True, stop=True)

        def quantize(codes, scales, grouped):
            nc.vector.quantize_mx(out=codes.bitcast(FP8X4), scales=scales, in_=grouped)

        def interleave(engine_copy, grouped, planes):
            engine_copy(out=grouped.rearrange("p (c i t) -> p c t i", i=4, t=PACK),
                        in_=planes.rearrange("p t (c i) -> p c t i", i=4))

        offs_sb = lists.tile([P, S // 16], U16, name="offs_sb")
        take_sb = lists.tile([P, V // 16], U16, name="take_sb")
        scale_table = sb.tile([P, T], U8, name="scale_table", tag="scales_then_wt", align_bytes=64)
        w1_raw = sb.tile([P, PACK, H], F32, name="w1_raw", align_bytes=64)

        nc.vector.memset(scale_table[:].bitcast(I32), 0)
        nc.scalar.dma_start(w1_raw[:], w1.rearrange("(p j) c -> p j c", j=PACK))
        nc.sync.dma_start(offs_sb[:], offs)
        nc.sync.dma_start(take_sb[:], take)
        for q in range(4):
            nc.sync.dma_start(scale_table[32 * q : 32 * q + 4, :].bitcast(I32), x_scales[0, 4 * q : 4 * q + 4, :].bitcast(I32))

        warm_in = sb.tile([P, 8], F32, name="warm_in", tag="warm_then_w2", align_bytes=64)
        warm_out = sb.tile([P, 8], F32, name="warm_out")
        nc.gpsimd.memset(warm_in[:], 0.0)
        nc.scalar.activation(warm_out[:], warm_in[:], SILU)

        z = [sb.tile([P, S], F32, name=f"z{t}", tag=f"z{t}", align_bytes=64) for t in range(PACK)]
        zeros = sb.tile([P, S], F32, name="zeros", tag="zeros_then_words", align_bytes=64)
        nc.vector.memset(zeros[:], 0.0)
        nc.vector.tensor_copy(out=z[0][:], in_=zeros[:])
        for t in range(1, PACK):
            nc.vector.memset(z[t][:], 0.0)
        word_table = sb.tile([P, T], U32, name="word_table", tag="zeros_then_words", align_bytes=64)
        nc.sync.dma_start(word_table[:].bitcast(I32), x_words[0].rearrange("p n t -> p (n t)").bitcast(I32))

        x_scale = sb.tile([P, S], U8, name="x_scale", align_bytes=64)
        nc.vector.tensor_copy(x_scale[:], scale_table[:].indirect(offs_sb[:]))

        w1_grouped = sb.tile([P, PACK, P, PACK], BF16, name="w1_grouped", align_bytes=64)
        w1_dst = w1_grouped[:].rearrange("p t m j -> p m j t")
        w1_src = w1_raw[:].rearrange("p j (m t) -> p m j t", t=PACK)
        nc.vector.tensor_copy(out=w1_dst[:, :W1_VECTOR_M, :, :2], in_=w1_src[:, :W1_VECTOR_M, :, :2])
        nc.scalar.copy(out=w1_dst[:, W1_VECTOR_M:, :, :2], in_=w1_src[:, W1_VECTOR_M:, :, :2])
        nc.scalar.copy(out=w1_dst[:, :, :, 2:], in_=w1_src[:, :, :, 2:])
        w1_codes = [sb.tile([P, 2, P], U32, name="w1_codes0", align_bytes=64),
                    sb.tile([P, 2, P], U32, name="w1_codes1", tag="zeros_then_words", align_bytes=64)]
        w1_scales = sb.tile([P, PACK, P], U8, name="w1_scales", align_bytes=64)

        def quantize_w1(h):
            pair = slice(2 * h, 2 * h + 2)
            quantize(w1_codes[h][:].rearrange("p t m -> p (t m)"), w1_scales[:, pair, :].rearrange("p t m -> p (t m)"),
                     w1_grouped[:, pair].rearrange("p t m j -> p (t m j)"))

        w2_raw = sb.tile([P, PACK, N], F32, name="w2_raw", tag="warm_then_w2", align_bytes=64)
        nc.sync.dma_start(w2_raw[:], w2.rearrange("(p j) c -> p j c", j=PACK))

        quantize_w1(0)
        x_codes = sb.tile([P, S], U32, name="x_codes", tag="x_codes_then_w2", align_bytes=64)
        for h in range(2):
            nc.vector.tensor_copy(x_codes[:, h * HALF : (h + 1) * HALF], word_table[:].indirect(offs_sb[:, h * HALF // 16 : (h + 1) * HALF // 16]))
        quantize_w1(1)

        wt_sb = sb.tile([P, V], F32, name="wt_sb", tag="scales_then_wt", align_bytes=64)
        nc.sync.dma_start(wt_sb[:], wt.rearrange("(p j) v -> p j v", j=PACK)[:, 0, :])

        act = [sb.tile([P, S], F32, name=f"act{t}", align_bytes=64) for t in range(PACK)]
        for bank, (t, c0, width) in enumerate(Y_PIECES):
            cols = slice(c0, c0 + width)
            y = psum.tile([P, width], F32, name=f"y{bank}", tag=f"bank{bank}")
            mx(y[:], w1_codes[t // 2][:, t % 2, :], w1_scales[:, t, :], x_codes[:, cols], x_scale[:, cols])
            nc.scalar.activation(act[t][:, cols], y[:], SILU)

        taken = [sb.tile([P, V], F32, name=f"taken{t}", align_bytes=64) for t in range(PACK)]
        for t in range(PACK):
            nc.vector.tensor_copy(taken[t][:], act[t][:].indirect(take_sb[:]))

        w2_grouped = [sb.tile([P, PACK * N // 2], BF16, name="w2_grouped0", tag="x_codes_then_w2", align_bytes=64),
                      sb.tile([P, PACK * N // 2], BF16, name="w2_grouped1", tag="z1", align_bytes=64)]
        w2_codes = [sb.tile([P, N // 2], U32, name=f"w2_codes{h}", align_bytes=64) for h in range(2)]
        w2_scales = [sb.tile([P, N // 2], U8, name=f"w2_scales{h}", align_bytes=64) for h in range(2)]
        z_grouped = [sb.tile([P, PACK * width], BF16, name=f"z_grouped{c}", align_bytes=64) for c, (c0, width) in enumerate(CHUNKS)]
        z_codes = [sb.tile([P, width], U32, name=f"z_codes{c}", align_bytes=64) for c, (c0, width) in enumerate(CHUNKS)]
        z_scales = [sb.tile([P, width], U8, name=f"z_scales{c}", align_bytes=64) for c, (c0, width) in enumerate(CHUNKS)]
        planes = [sb.tile([P, PACK, width], BF16, name=f"planes{c}", align_bytes=64) for c, (c0, width) in enumerate(CHUNKS) if c > 0]
        first_slots = z_grouped[0][:].rearrange("p (c t) -> p c t", t=PACK)

        def interleave_w2(h):
            interleave(nc.scalar.copy, w2_grouped[h][:], w2_raw[:, :, h * N // 2 : (h + 1) * N // 2])

        def round_plane(t, c):
            c0, width = CHUNKS[c]
            nc.scalar.copy(out=planes[c - 1][:, t, :], in_=z[t][:, c0 : c0 + width])

        for t in range(PACK):
            nc.vector.tensor_tensor(z[t][:].indirect(take_sb[:]), taken[t][:], wt_sb[:], MULT)
        interleave_w2(0)
        for t in (0, 1):
            nc.scalar.copy(out=first_slots[:, :, t], in_=z[t][:, :P])
            round_plane(t, 1)
            round_plane(t, 2)
        interleave_w2(1)
        for t in (2, 3):
            nc.vector.tensor_copy(out=first_slots[:, :, t], in_=z[t][:, :P])
        round_plane(2, 1)
        round_plane(2, 2)
        round_plane(3, 1)
        interleave(nc.scalar.copy, z_grouped[1][:], planes[0][:])
        round_plane(3, 2)

        quantize(w2_codes[0][:], w2_scales[0][:], w2_grouped[0][:])
        quantize(z_codes[0][:], z_scales[0][:], z_grouped[0][:])
        quantize(w2_codes[1][:], w2_scales[1][:], w2_grouped[1][:])
        quantize(z_codes[1][:], z_scales[1][:], z_grouped[1][:])
        interleave(nc.scalar.copy, z_grouped[2][:, PACK * LAST_VECTOR_COLS :], planes[1][:, :, LAST_VECTOR_COLS:])
        interleave(nc.vector.tensor_copy, z_grouped[2][:, : PACK * LAST_VECTOR_COLS], planes[1][:, :, :LAST_VECTOR_COLS])
        quantize(z_codes[2][:], z_scales[2][:], z_grouped[2][:])

        out_rows = out.rearrange("(u p) s -> p u s", p=P)
        pieces = [(0, 0, 1, 0, P), (0, 1, 1, 0, P), (0, 2, 2, 0, P), (1, 0, 2, 0, P), (1, 2, 2, 0, P),
                  (2, 0, 1, 0, HALF), (2, 1, 1, 0, HALF), (2, 2, 1, 0, HALF), (2, 3, 1, 0, P), (2, 3, 1, P, P)]
        for n, (c, u0, tiles, lo, width) in enumerate(pieces):
            acc = psum.tile([P, tiles, width], F32, name=f"acc{n}", tag=f"bank{n % 8}")
            for i in range(tiles):
                h, m0 = divmod((u0 + i) * P, N // 2)
                mx(acc[:, i, :], w2_codes[h][:, m0 : m0 + P], w2_scales[h][:, m0 : m0 + P],
                   z_codes[c][:, lo : lo + width], z_scales[c][:, lo : lo + width])
            staged = sb.tile([P, tiles, width], F32, name=f"staged{n}")
            if n < 4 or n % 2 == 1:
                nc.scalar.copy(out=staged[:], in_=acc[:])
            else:
                nc.vector.tensor_copy(out=staged[:], in_=acc[:])
            c0 = CHUNKS[c][0] + lo
            nc.sync.dma_start(out_rows[:, u0 : u0 + tiles, c0 : c0 + width], staged[:])
